import numpy as np
import ml_dtypes


def mxq(x, axis, fmt="e4m3"):
    dtype, down = {"e4m3": (ml_dtypes.float8_e4m3fn, 7), "e5m2": (ml_dtypes.float8_e5m2, 14)}[fmt]
    v = np.moveaxis(np.asarray(x, np.float32).astype(ml_dtypes.bfloat16).astype(np.float64), axis, -1)
    blocks = v.reshape(v.shape[:-1] + (-1, 32))
    amax = np.abs(blocks).max(-1, keepdims=True)
    byte = np.maximum(np.where(amax > 0, np.frexp(amax)[1] - 1 + 127, 0) - down, 1)
    scale = np.exp2(byte - 127.0)
    codes = (blocks / scale).astype(np.float32).astype(dtype).astype(np.float64)
    return np.moveaxis((codes * scale).reshape(v.shape), -1, axis)


WIDE = False


def mx_kscale(k):
    if not WIDE:
        return np.ones(k)
    levels = np.array([10, -10, 5, -5, 0])
    if k % 512:
        return np.exp2(np.random.permutation(np.resize(levels, k // 32))).repeat(32)
    a = np.empty((k // 512, 16))
    for p in range(k // 512):
        a[p, :8] = np.random.permutation(np.resize(levels, 8))
        for g in range(8):
            far = levels[np.abs(levels - a[p, g]) >= 10]
            a[p, g + 8] = far[np.random.randint(len(far))]
    return np.exp2(a.ravel()).repeat(32)


def f64(x):
    return np.asarray(x).astype(np.float64)


def striped8(idx):
    return np.asarray(idx).reshape(8, -1, 16).transpose(0, 2, 1).reshape(128, -1).astype(np.uint16)


def unstriped8(offs):
    return offs.reshape(8, 16, -1).transpose(0, 2, 1).reshape(8, -1).astype(np.int64)


def pick8(x, idx, run):
    r = np.arange(len(x))
    return x[r[:, None], idx[r % (8 * run) // run]]


E2M1 = np.array([0.0, 0.5, 1.0, 1.5, 2.0, 3.0, 4.0, 6.0, -0.0, -0.5, -1.0, -1.5, -2.0, -3.0, -4.0, -6.0])


def pack_weight(w, fmt):
    k, n = w.shape
    w = f64(np.asarray(w, np.float32).astype(ml_dtypes.bfloat16)).reshape(k // 32, 32, n)
    amax = np.abs(w).max(1)
    if fmt == "e4m3":
        byte = np.frexp(amax)[1] - 1 + 127 - 7
    else:
        mant, ex = np.frexp(amax / 6.0)
        byte = np.where(mant > 0.5, ex, ex - 1) + 127
    byte = np.clip(np.where(amax > 0, byte, 1), 1, 254)
    scaled = (w * np.exp2(127.0 - byte)[:, None, :]).reshape(k, n).astype(np.float32)
    by_word = np.ascontiguousarray(scaled.reshape(k // 512, 128, 4, n).transpose(0, 1, 3, 2))
    if fmt == "e4m3":
        words = by_word.astype(ml_dtypes.float8_e4m3fn).view(np.uint8)
    else:
        c = by_word.astype(ml_dtypes.float4_e2m1fn).view(np.uint8) & 0xF
        words = (c[..., 0::2] | (c[..., 1::2] << 4)).reshape(k // 512, 128, 2 * n)
    return np.ascontiguousarray(words), np.ascontiguousarray(byte.astype(np.uint8).reshape(k // 512, 16, n))


def unpack_weight(words, scales, fmt):
    g, _, n = scales.shape
    words = np.ascontiguousarray(words).reshape(g, 128, n, -1)
    if fmt == "e4m3":
        vals = words.view(ml_dtypes.float8_e4m3fn).astype(np.float64)
    else:
        nib = np.empty((g, 128, n, 4), np.uint8)
        nib[..., 0::2] = words & 0xF
        nib[..., 1::2] = words >> 4
        vals = E2M1[nib]
    vals = vals * np.repeat(np.exp2(scales.astype(np.float64) - 127.0), 8, axis=1)[..., None]
    return vals.transpose(0, 1, 3, 2).reshape(g * 512, n)


D, T, U, X, I, Q, E = 512, 1024, 1024, 1024, 512, 512, 256


def setup_inputs():
    n = np.random.standard_normal
    idx = np.stack([np.random.permutation(T)[:I] for _ in range(8)])
    idx2 = np.stack([np.random.permutation(X)[:I] for _ in range(8)])
    idx3 = np.stack([np.random.permutation(U)[:I] for _ in range(8)])
    idx4 = np.stack([np.random.permutation(X)[:I] for _ in range(8)])
    idx5 = np.stack([np.random.permutation(X)[:I] for _ in range(8)])
    fd = mx_kscale(D)
    fq = mx_kscale(Q)
    keysp = pack_weight(n((D, T)) / fd[:, None], "e4m3")
    notesp = pack_weight(n((D, U)) / fd[:, None], "e2m1")
    usersp = pack_weight(n((D, X)) / fd[:, None], "e2m1")
    mixp = pack_weight(n((Q, E)) * 1.0 / np.sqrt(Q) / fq[:, None], "e2m1")
    return {
        "query": (n((D, Q)) * 1.0 / np.sqrt(D) * fd[:, None]).astype(np.float32),
        "query2": (n((D, Q)) * 1.0 / np.sqrt(D) * fd[:, None]).astype(np.float32),
        "keys_words": keysp[0],
        "keys_scales": keysp[1],
        "notes_words": notesp[0],
        "notes_scales": notesp[1],
        "users_words": usersp[0],
        "users_scales": usersp[1],
        "lam": (np.random.uniform(0.5, 1.5, (Q, 1))).astype(np.float32),
        "rowf": (np.random.uniform(0.5, 2.0, (Q, 1)) * fq[:, None]).astype(np.float32),
        "mix_words": mixp[0],
        "mix_scales": mixp[1],
        "offs": striped8(idx),
        "offs2": striped8(idx2),
        "offs3": striped8(idx3),
        "offs4": striped8(idx4),
        "offs5": striped8(idx5),
    }


def reference(query, query2, keys_words, keys_scales, notes_words, notes_scales, users_words, users_scales, lam, rowf, mix_words, mix_scales, offs, offs2, offs3, offs4, offs5):
    idx = unstriped8(offs)
    idx2 = unstriped8(offs2)
    idx3 = unstriped8(offs3)
    idx4 = unstriped8(offs4)
    idx5 = unstriped8(offs5)
    keysu = unpack_weight(keys_words, keys_scales, "e4m3")
    notesu = unpack_weight(notes_words, notes_scales, "e2m1")
    usersu = unpack_weight(users_words, users_scales, "e2m1")
    mixu = unpack_weight(mix_words, mix_scales, "e2m1")
    queryq = mxq(f64(query), 0, "e4m3")
    a = queryq.T @ keysu
    b = queryq.T @ notesu
    query2q = mxq(f64(query2), 0, "e4m3")
    c0 = query2q.T @ usersu
    f1 = np.zeros((Q, X))
    f1[np.arange(Q)[:, None], idx2[np.arange(Q) % 512 // 64]] = pick8(a, idx, 64)
    f2 = np.zeros((Q, X))
    f2[np.arange(Q)[:, None], idx4[np.arange(Q) % 512 // 64]] = pick8(b, idx3, 64)
    r = np.maximum(f1, f2 * f64(lam))
    cc = c0 + r
    g = pick8(cc, idx5, 64)
    gw = g * f64(rowf)
    gwq = mxq(gw, 0, "e4m3")
    y = mixu.T @ gwq
    return y

@@ -1,0 +1,258 @@
+from contextlib import ExitStack
+
+import concourse.mybir as mybir
+
+D, T, I, Q, E = 512, 1024, 512, 512, 256
+FLOPS = 2 * D * Q * T * 3 + 2 * Q * E * I
+
+F32 = mybir.dt.float32
+BF16 = mybir.dt.bfloat16
+I32 = mybir.dt.int32
+U32 = mybir.dt.uint32
+U16 = mybir.dt.uint16
+U8 = mybir.dt.uint8
+FP8X4 = mybir.dt.float8_e4m3fn_x4
+FP4X4 = mybir.dt.float4_e2m1fn_x4
+COPY = mybir.ActivationFunctionType.Copy
+MULT = mybir.AluOpType.mult
+ADD = mybir.AluOpType.add
+MAX = mybir.AluOpType.max
+
+P = 128
+PACK = 4
+BANK = 512
+HALF = I // 2
+LAST = PACK - 1
+
+
+def tile_attend_twocourts_threeq_mixed_kernel(
+    tc, query, query2, keys_words, keys_scales, notes_words, notes_scales, users_words, users_scales,
+    lam, rowf, mix_words, mix_scales, offs, offs2, offs3, offs4, offs5, out,
+):
+    nc = tc.nc
+    with ExitStack() as ctx:
+        held = ctx.enter_context(tc.tile_pool(name="held", bufs=1))
+        ring4 = ctx.enter_context(tc.tile_pool(name="ring4", bufs=4))
+        psum = ctx.enter_context(tc.psum_pool(name="psum", bufs=1))
+        turn_banks = [psum.tile([P, BANK], F32, name="turn%d" % k) for k in range(2)]
+        last_banks = [psum.tile([P, BANK], F32, name="last%d" % k) for k in range(2)]
+
+        def load_list(src, name):
+            tile = held.tile([P, I // 16], U16, name=name)
+            nc.sync.dma_start(tile[:], src)
+            return tile
+
+        def zeroed_scales(width, name, engine):
+            tile = held.tile([P, width], U8, name=name, align_bytes=64)
+            engine.memset(tile[:].bitcast(I32), 0)
+            return tile
+
+        def load_scales(tile, src):
+            for quad in range(4):
+                nc.sync.dma_start(
+                    tile[32 * quad : 32 * quad + 4, :].bitcast(I32), src[0, 4 * quad : 4 * quad + 4, :].bitcast(I32)
+                )
+
+        def load_fp4_words(src, width, name):
+            tile = held.tile([P, 2 * width], U8, name=name, align_bytes=64)
+            nc.sync.dma_start(tile[:].bitcast(I32), src[0].bitcast(I32))
+            return tile
+
+        def load_query_half(src, half, name):
+            tile = held.tile([P, PACK, Q // 2], F32, name=name)
+            nc.sync.dma_start(
+                tile[:], src.rearrange("(p j) q -> p j q", j=PACK)[:, :, half * (Q // 2) : (half + 1) * (Q // 2)]
+            )
+            return tile
+
+        notes_s = zeroed_scales(T, "notes_s", nc.gpsimd)
+        keys_s = zeroed_scales(T, "keys_s", nc.vector)
+        users_s = zeroed_scales(T, "users_s", nc.vector)
+        mix_s = zeroed_scales(E, "mix_s", nc.vector)
+        f1 = [held.tile([P, T], F32, name="f1_%d" % k) for k in range(2)]
+        f2 = [held.tile([P, T], F32, name="f2_%d" % k) for k in range(2)]
+        nc.vector.memset(f2[0][:], 0.0)
+        nc.gpsimd.memset(f1[0][:], 0.0)
+        nc.gpsimd.memset(f2[1][:], 0.0)
+        nc.gpsimd.memset(f1[1][:], 0.0)
+
+        list3 = load_list(offs3, "list3")
+        list4 = load_list(offs4, "list4")
+        q_raw = [load_query_half(query, half, "q_raw%d" % half) for half in range(2)]
+        notes_w = load_fp4_words(notes_words, T, "notes_w")
+        load_scales(notes_s, notes_scales)
+        keys_w = held.tile([P, T], U32, name="keys_w", align_bytes=64)
+        nc.sync.dma_start(keys_w[:].bitcast(I32), keys_words[0].rearrange("p n r -> p (n r)").bitcast(I32))
+        load_scales(keys_s, keys_scales)
+        list1 = load_list(offs, "list1")
+        list2 = load_list(offs2, "list2")
+        q2_raw = [load_query_half(query2, half, "q2_raw%d" % half) for half in range(2)]
+        lam_sb = held.tile([P, PACK], F32, name="lam_sb")
+        nc.sync.dma_start(lam_sb[:], lam.rearrange("(p t) o -> p (t o)", t=PACK))
+        users_w = load_fp4_words(users_words, T, "users_w")
+        load_scales(users_s, users_scales)
+        list5 = load_list(offs5, "list5")
+        rowf_sb = held.tile([P, PACK], F32, name="rowf_sb")
+        nc.sync.dma_start(rowf_sb[:], rowf.rearrange("(p t) o -> p (t o)", t=PACK))
+        mix_w = load_fp4_words(mix_words, E, "mix_w")
+        load_scales(mix_s, mix_scales)
+
+        q_first = held.tile([P, P, PACK], BF16, name="q_first", align_bytes=64)
+        q_rest = held.tile([P, LAST, P, PACK], BF16, name="q_rest", align_bytes=64)
+        r = held.tile([P, T], F32, name="r", align_bytes=64)
+        q2_all = r[:].bitcast(BF16).rearrange("p (t m j) -> p t m j", t=PACK, j=PACK)
+        for half in range(2):
+            ms = slice(half * 64, (half + 1) * 64)
+            dealt = q_raw[half][:].rearrange("p j (m t) -> p m t j", t=PACK)
+            nc.vector.tensor_copy(q_first[:, ms, :], dealt[:, :, 0, :])
+            nc.scalar.copy(q_rest[:, :, ms, :].rearrange("p t m j -> p m t j"), dealt[:, :, 1:PACK, :])
+        first_c = held.tile([P, P], U32, name="first_c", align_bytes=64)
+        first_s = held.tile([P, P], U8, name="first_s", align_bytes=64)
+        rest_c = held.tile([P, LAST * P], U32, name="rest_c", align_bytes=64)
+        rest_s = held.tile([P, LAST * P], U8, name="rest_s", align_bytes=64)
+        nc.vector.quantize_mx(first_c[:].bitcast(FP8X4), first_s[:], q_first[:].rearrange("p m j -> p (m j)"))
+        nc.vector.quantize_mx(rest_c[:].bitcast(FP8X4), rest_s[:], q_rest[:].rearrange("p t m j -> p (t m j)"))
+        q_ops = [(first_c[:], first_s[:])] + [
+            (rest_c[:, k * P : (k + 1) * P], rest_s[:, k * P : (k + 1) * P]) for k in range(LAST)
+        ]
+        q2_c = held.tile([P, Q], U32, name="q2_c", align_bytes=64)
+        q2_s = held.tile([P, Q], U8, name="q2_s", align_bytes=64)
+
+        def quantise_query2():
+            for half in range(2):
+                ms = slice(half * 64, (half + 1) * 64)
+                nc.gpsimd.tensor_scalar(
+                    q2_all[:, :, ms, :].rearrange("p t m j -> p m t j"),
+                    q2_raw[half][:].rearrange("p j (m t) -> p m t j", t=PACK),
+                    1.0, 0.0, MULT, ADD,
+                )
+            nc.vector.quantize_mx(q2_c[:].bitcast(FP8X4), q2_s[:], r[:].bitcast(BF16))
+
+        def scores(banks, rows, words, scales):
+            for k in range(2):
+                nc.tensor.matmul_mx(
+                    banks[k][:], lhsT=rows[0].bitcast(FP8X4), lhsT_scale=rows[1],
+                    rhs=words(k), rhs_scale=scales[:, k * BANK : (k + 1) * BANK], start=True, stop=True,
+                )
+
+        def notes_cols(k):
+            return notes_w[:, 2 * k * BANK : 2 * (k + 1) * BANK].bitcast(FP4X4)
+
+        def users_cols(k):
+            return users_w[:, 2 * k * BANK : 2 * (k + 1) * BANK].bitcast(FP4X4)
+
+        def keys_cols(k):
+            return keys_w[:, k * BANK : (k + 1) * BANK].bitcast(FP8X4)
+
+        a_sb = held.tile([P, T], F32, name="a_sb")
+        b_sb = held.tile([P, T], F32, name="b_sb")
+        c0 = held.tile([P, T], F32, name="c0")
+        cc_tiles = [held.tile([P, T], F32, name="cc%d" % k) for k in range(2)]
+        slots = [held.tile([P, I], F32, name="slots%d" % k) for k in range(10)]
+        b_picked = slots[0:4]
+        a_picked = slots[4:8]
+        g_tiles = [slots[6], slots[7], slots[8], slots[9]]
+
+        def pick(t, words, scales, whole, picked, pick_list, shared):
+            banks = turn_banks
+            scores(banks, q_ops[t], words, scales)
+            nc.scalar.copy(whole[:, :BANK], banks[0][:])
+            if shared:
+                nc.vector.tensor_copy(whole[:, BANK:], banks[1][:])
+                nc.scalar.activation(picked[:, :HALF], whole[:].indirect(pick_list[:, :16]), COPY)
+                nc.scalar.activation(picked[:, HALF:], whole[:].indirect(pick_list[:, 16:]), COPY)
+            else:
+                nc.scalar.copy(whole[:, BANK:], banks[1][:])
+                nc.scalar.activation(picked[:], whole[:].indirect(pick_list[:]), COPY)
+
+        def pick_notes(t):
+            pick(t, notes_cols, notes_s, b_sb, b_picked[t], list3, t == 0)
+
+        def pick_keys(t):
+            pick(t, keys_cols, keys_s, a_sb, a_picked[t], list1, False)
+
+        def put(t):
+            k = 1 if t == 2 else 0
+            if t == 0:
+                for half in range(2):
+                    nc.vector.tensor_copy(
+                        f2[k][:].indirect(list4[:, 16 * half : 16 * (half + 1)]),
+                        b_picked[t][:, half * HALF : (half + 1) * HALF],
+                    )
+            else:
+                nc.vector.tensor_copy(f2[k][:].indirect(list4[:]), b_picked[t][:])
+            nc.vector.tensor_copy(f1[k][:].indirect(list2[:]), a_picked[t][:])
+            pieces = 2 if t == LAST else 1
+            for piece in range(pieces):
+                cols = slice(piece * T // pieces, (piece + 1) * T // pieces)
+                nc.vector.scalar_tensor_tensor(
+                    r[:, cols], f2[k][:, cols], lam_sb[:, t : t + 1], f1[k][:, cols], MULT, MAX
+                )
+
+        def add_users(t):
+            rows = (q2_c[:, t * P : (t + 1) * P], q2_s[:, t * P : (t + 1) * P])
+            banks = last_banks if t == LAST else turn_banks
+            scores(banks, rows, users_cols, users_s)
+            cc = cc_tiles[t // LAST]
+            if t == LAST:
+                for k in range(2):
+                    cols = slice(k * BANK, (k + 1) * BANK)
+                    nc.vector.tensor_tensor(cc[:, cols], r[:, cols], banks[k][:], ADD)
+            else:
+                for k in range(2):
+                    nc.scalar.copy(c0[:, k * BANK : (k + 1) * BANK], banks[k][:])
+                nc.gpsimd.tensor_tensor(cc[:], r[:], c0[:], ADD)
+
+        gw = [held.tile([P, HALF, PACK], BF16, name="gw%d" % half, align_bytes=64) for half in range(2)]
+
+        def weigh(t):
+            factor = rowf_sb[:, t : t + 1]
+            g = g_tiles[t]
+            cc = cc_tiles[t // LAST]
+            if t == LAST:
+                nc.vector.tensor_copy(g[:, :HALF], cc[:].indirect(list5[:, :16]))
+                nc.scalar.activation(g[:, HALF:], cc[:].indirect(list5[:, 16:]), COPY)
+            else:
+                nc.scalar.activation(g[:], cc[:].indirect(list5[:]), COPY)
+            if t >= 2:
+                nc.vector.tensor_scalar(gw[0][:, :, t], g[:, :HALF], factor, None, MULT)
+                nc.scalar.activation(gw[1][:, :, t], g[:, HALF:], COPY, scale=factor)
+            else:
+                for half in range(2):
+                    nc.gpsimd.tensor_scalar(
+                        gw[half][:, :, t], g[:, half * HALF : (half + 1) * HALF], factor, 0.0, MULT, ADD
+                    )
+
+        pick_notes(0)
+        pick_keys(0)
+        quantise_query2()
+        for t in range(PACK):
+            put(t)
+            if t < LAST:
+                pick_notes(t + 1)
+            if t > 0:
+                weigh(t - 1)
+            if t < LAST:
+                pick_keys(t + 1)
+            add_users(t)
+        weigh(LAST)
+
+        for half in range(2):
+            gw_c = held.tile([P, HALF], U32, name="gw_c%d" % half, align_bytes=64)
+            gw_s = held.tile([P, HALF], U8, name="gw_s%d" % half, align_bytes=64)
+            nc.vector.quantize_mx(gw_c[:].bitcast(FP8X4), gw_s[:], gw[half][:].rearrange("p i t -> p (i t)"))
+            for c in range(E // P):
+                bank = psum.tile([P, HALF], F32, name="y_bank%d%d" % (half, c))
+                nc.tensor.matmul_mx(
+                    bank[:], lhsT=mix_w[:, 2 * c * P : 2 * (c + 1) * P].bitcast(FP4X4),
+                    lhsT_scale=mix_s[:, c * P : (c + 1) * P],
+                    rhs=gw_c[:].bitcast(FP8X4), rhs_scale=gw_s[:], start=True, stop=True,
+                )
+                y = ring4.tile([P, HALF], F32, name="y")
+                place = out[c * P : (c + 1) * P, half * HALF : (half + 1) * HALF]
+                if c == half:
+                    nc.scalar.copy(y[:], bank[:])
+                    nc.scalar.dma_start(place, y[:])
+                else:
+                    nc.vector.tensor_copy(y[:], bank[:])
+                    nc.sync.dma_start(place, y[:])

@@ -59,7 +59,7 @@ def tile_attend_twocourts_threeq_mixed_kernel(
             return tile
 
         def load_query_half(src, half, name):
-            tile = held.tile([P, PACK, Q // 2], F32, name=name)
+            tile = held.tile([P, PACK, Q // 2], F32, name=name, tag=name)
             nc.sync.dma_start(
                 tile[:], src.rearrange("(p j) q -> p j q", j=PACK)[:, :, half * (Q // 2) : (half + 1) * (Q // 2)]
             )
@@ -69,18 +69,16 @@ def tile_attend_twocourts_threeq_mixed_kernel(
         keys_s = zeroed_scales(T, "keys_s", nc.vector)
         users_s = zeroed_scales(T, "users_s", nc.vector)
         mix_s = zeroed_scales(E, "mix_s", nc.vector)
-        f1 = [held.tile([P, T], F32, name="f1_%d" % k) for k in range(2)]
-        f2 = [held.tile([P, T], F32, name="f2_%d" % k) for k in range(2)]
+        f1 = held.tile([P, T], F32, name="f1")
+        f2 = [held.tile([P, T], F32, name="f2_first")]
         nc.vector.memset(f2[0][:], 0.0)
-        nc.gpsimd.memset(f1[0][:], 0.0)
-        nc.gpsimd.memset(f2[1][:], 0.0)
-        nc.gpsimd.memset(f1[1][:], 0.0)
+        nc.gpsimd.memset(f1[:], 0.0)
 
-        list3 = load_list(offs3, "list3")
-        list4 = load_list(offs4, "list4")
         q_raw = [load_query_half(query, half, "q_raw%d" % half) for half in range(2)]
         notes_w = load_fp4_words(notes_words, T, "notes_w")
         load_scales(notes_s, notes_scales)
+        list3 = load_list(offs3, "list3")
+        list4 = load_list(offs4, "list4")
         keys_w = held.tile([P, T], U32, name="keys_w", align_bytes=64)
         nc.sync.dma_start(keys_w[:].bitcast(I32), keys_words[0].rearrange("p n r -> p (n r)").bitcast(I32))
         load_scales(keys_s, keys_scales)
@@ -127,6 +125,8 @@ def tile_attend_twocourts_threeq_mixed_kernel(
                     1.0, 0.0, MULT, ADD,
                 )
             nc.vector.quantize_mx(q2_c[:].bitcast(FP8X4), q2_s[:], r[:].bitcast(BF16))
+            f2.append(held.tile([P, T], F32, name="f2_second", tag="q2_raw1"))
+            nc.gpsimd.memset(f2[1][:], 0.0)
 
         def scores(banks, rows, words, scales):
             for k in range(2):
@@ -146,62 +146,70 @@ def tile_attend_twocourts_threeq_mixed_kernel(
 
         a_sb = held.tile([P, T], F32, name="a_sb")
         b_sb = held.tile([P, T], F32, name="b_sb")
-        c0 = held.tile([P, T], F32, name="c0")
+        c0 = [held.tile([P, T], F32, name="c0_%d" % k) for k in range(2)]
         cc_tiles = [held.tile([P, T], F32, name="cc%d" % k) for k in range(2)]
-        slots = [held.tile([P, I], F32, name="slots%d" % k) for k in range(10)]
+        slots = [held.tile([P, I], F32, name="slots%d" % k) for k in range(9)]
         b_picked = slots[0:4]
         a_picked = slots[4:8]
-        g_tiles = [slots[6], slots[7], slots[8], slots[9]]
+        g_tiles = [slots[6], slots[7], slots[8], slots[8]]
 
-        def pick(t, words, scales, whole, picked, pick_list, shared):
-            banks = turn_banks
-            scores(banks, q_ops[t], words, scales)
-            nc.scalar.copy(whole[:, :BANK], banks[0][:])
-            if shared:
-                nc.vector.tensor_copy(whole[:, BANK:], banks[1][:])
-                nc.scalar.activation(picked[:, :HALF], whole[:].indirect(pick_list[:, :16]), COPY)
-                nc.scalar.activation(picked[:, HALF:], whole[:].indirect(pick_list[:, 16:]), COPY)
-            else:
-                nc.scalar.copy(whole[:, BANK:], banks[1][:])
-                nc.scalar.activation(picked[:], whole[:].indirect(pick_list[:]), COPY)
+        def empty(banks, whole):
+            for k in range(2):
+                nc.scalar.copy(whole[:, k * BANK : (k + 1) * BANK], banks[k][:])
 
         def pick_notes(t):
-            pick(t, notes_cols, notes_s, b_sb, b_picked[t], list3, t == 0)
+            if t == 0:
+                quarter = T // 4
+                for k, bank in enumerate(turn_banks + last_banks):
+                    cols = slice(k * quarter, (k + 1) * quarter)
+                    nc.tensor.matmul_mx(
+                        bank[:, :quarter], lhsT=q_ops[t][0].bitcast(FP8X4), lhsT_scale=q_ops[t][1],
+                        rhs=notes_w[:, 2 * k * quarter : 2 * (k + 1) * quarter].bitcast(FP4X4),
+                        rhs_scale=notes_s[:, cols], start=True, stop=True,
+                    )
+                    if k % 2 == 0:
+                        nc.scalar.copy(b_sb[:, cols], bank[:, :quarter])
+                    else:
+                        nc.vector.tensor_copy(b_sb[:, cols], bank[:, :quarter])
+                nc.scalar.activation(b_picked[t][:, :HALF], b_sb[:].indirect(list3[:, :16]), COPY)
+                nc.vector.tensor_copy(b_picked[t][:, HALF:], b_sb[:].indirect(list3[:, 16:]))
+            else:
+                scores(turn_banks, q_ops[t], notes_cols, notes_s)
+                empty(turn_banks, b_sb)
+                nc.scalar.activation(b_picked[t][:], b_sb[:].indirect(list3[:]), COPY)
+
+        def score_keys(t):
+            scores(turn_banks, q_ops[t], keys_cols, keys_s)
+            empty(turn_banks, a_sb)
 
         def pick_keys(t):
-            pick(t, keys_cols, keys_s, a_sb, a_picked[t], list1, False)
+            nc.scalar.activation(a_picked[t][:], a_sb[:].indirect(list1[:]), COPY)
 
         def put(t):
             k = 1 if t == 2 else 0
-            if t == 0:
-                for half in range(2):
-                    nc.vector.tensor_copy(
-                        f2[k][:].indirect(list4[:, 16 * half : 16 * (half + 1)]),
-                        b_picked[t][:, half * HALF : (half + 1) * HALF],
-                    )
-            else:
-                nc.vector.tensor_copy(f2[k][:].indirect(list4[:]), b_picked[t][:])
-            nc.vector.tensor_copy(f1[k][:].indirect(list2[:]), a_picked[t][:])
+            nc.vector.tensor_copy(f2[k][:].indirect(list4[:]), b_picked[t][:])
+            nc.vector.tensor_copy(f1[:].indirect(list2[:]), a_picked[t][:])
             pieces = 2 if t == LAST else 1
             for piece in range(pieces):
                 cols = slice(piece * T // pieces, (piece + 1) * T // pieces)
                 nc.vector.scalar_tensor_tensor(
-                    r[:, cols], f2[k][:, cols], lam_sb[:, t : t + 1], f1[k][:, cols], MULT, MAX
+                    r[:, cols], f2[k][:, cols], lam_sb[:, t : t + 1], f1[:, cols], MULT, MAX
                 )
 
-        def add_users(t):
+        def score_users(t):
             rows = (q2_c[:, t * P : (t + 1) * P], q2_s[:, t * P : (t + 1) * P])
-            banks = last_banks if t == LAST else turn_banks
-            scores(banks, rows, users_cols, users_s)
+            scores(last_banks if t == LAST else turn_banks, rows, users_cols, users_s)
+            if t < LAST:
+                empty(turn_banks, c0[t % 2])
+
+        def add_users(t):
             cc = cc_tiles[t // LAST]
             if t == LAST:
                 for k in range(2):
                     cols = slice(k * BANK, (k + 1) * BANK)
-                    nc.vector.tensor_tensor(cc[:, cols], r[:, cols], banks[k][:], ADD)
+                    nc.vector.tensor_tensor(cc[:, cols], r[:, cols], last_banks[k][:], ADD)
             else:
-                for k in range(2):
-                    nc.scalar.copy(c0[:, k * BANK : (k + 1) * BANK], banks[k][:])
-                nc.gpsimd.tensor_tensor(cc[:], r[:], c0[:], ADD)
+                nc.gpsimd.tensor_tensor(cc[:], r[:], c0[t % 2][:], ADD)
 
         gw = [held.tile([P, HALF, PACK], BF16, name="gw%d" % half, align_bytes=64) for half in range(2)]
 
@@ -212,29 +220,36 @@ def tile_attend_twocourts_threeq_mixed_kernel(
             if t == LAST:
                 nc.vector.tensor_copy(g[:, :HALF], cc[:].indirect(list5[:, :16]))
                 nc.scalar.activation(g[:, HALF:], cc[:].indirect(list5[:, 16:]), COPY)
+                nc.vector.tensor_scalar(gw[0][:, :, t], g[:, :HALF], factor, None, MULT)
+                nc.scalar.activation(gw[1][:, :P, t], g[:, HALF : HALF + P], COPY, scale=factor)
+                nc.vector.tensor_scalar(gw[1][:, P:, t], g[:, HALF + P :], factor, None, MULT)
             else:
                 nc.scalar.activation(g[:], cc[:].indirect(list5[:]), COPY)
-            if t >= 2:
-                nc.vector.tensor_scalar(gw[0][:, :, t], g[:, :HALF], factor, None, MULT)
-                nc.scalar.activation(gw[1][:, :, t], g[:, HALF:], COPY, scale=factor)
-            else:
                 for half in range(2):
                     nc.gpsimd.tensor_scalar(
                         gw[half][:, :, t], g[:, half * HALF : (half + 1) * HALF], factor, 0.0, MULT, ADD
                     )
 
         pick_notes(0)
+        score_keys(0)
         pick_keys(0)
         quantise_query2()
-        for t in range(PACK):
-            put(t)
-            if t < LAST:
-                pick_notes(t + 1)
-            if t > 0:
-                weigh(t - 1)
-            if t < LAST:
-                pick_keys(t + 1)
+        put(0)
+        pick_notes(1)
+        score_keys(1)
+        pick_keys(1)
+        score_users(0)
+        for t in range(LAST):
             add_users(t)
+            put(t + 1)
+            if t + 2 < PACK:
+                pick_notes(t + 2)
+                score_keys(t + 2)
+            score_users(t + 1)
+            weigh(t)
+            if t + 2 < PACK:
+                pick_keys(t + 2)
+        add_users(LAST)
         weigh(LAST)
 
         for half in range(2):

@@ -148,10 +148,10 @@ def tile_attend_twocourts_threeq_mixed_kernel(
         b_sb = held.tile([P, T], F32, name="b_sb")
         c0 = [held.tile([P, T], F32, name="c0_%d" % k) for k in range(2)]
         cc_tiles = [held.tile([P, T], F32, name="cc%d" % k) for k in range(2)]
-        slots = [held.tile([P, I], F32, name="slots%d" % k) for k in range(9)]
+        slots = [held.tile([P, I], F32, name="slots%d" % k) for k in range(11)]
         b_picked = slots[0:4]
         a_picked = slots[4:8]
-        g_tiles = [slots[6], slots[7], slots[8], slots[8]]
+        g_tiles = [slots[8], slots[9], slots[10], slots[10]]
 
         def empty(banks, whole):
             for k in range(2):
@@ -225,10 +225,12 @@ def tile_attend_twocourts_threeq_mixed_kernel(
                 nc.vector.tensor_scalar(gw[1][:, P:, t], g[:, HALF + P :], factor, None, MULT)
             else:
                 nc.scalar.activation(g[:], cc[:].indirect(list5[:]), COPY)
-                for half in range(2):
-                    nc.gpsimd.tensor_scalar(
-                        gw[half][:, :, t], g[:, half * HALF : (half + 1) * HALF], factor, 0.0, MULT, ADD
-                    )
+
+        def weigh_early(t):
+            for half in range(2):
+                nc.gpsimd.tensor_scalar(
+                    gw[half][:, :, t], g_tiles[t][:, half * HALF : (half + 1) * HALF], rowf_sb[:, t : t + 1], 0.0, MULT, ADD
+                )
 
         pick_notes(0)
         score_keys(0)
@@ -241,14 +243,16 @@ def tile_attend_twocourts_threeq_mixed_kernel(
         score_users(0)
         for t in range(LAST):
             add_users(t)
+            if t > 0:
+                weigh_early(t - 1)
             put(t + 1)
             if t + 2 < PACK:
                 pick_notes(t + 2)
                 score_keys(t + 2)
+                pick_keys(t + 2)
             score_users(t + 1)
             weigh(t)
-            if t + 2 < PACK:
-                pick_keys(t + 2)
+        weigh_early(LAST - 1)
         add_users(LAST)
         weigh(LAST)
 

from contextlib import ExitStack

import concourse.mybir as mybir

D, T, I, Q, E = 512, 1024, 512, 512, 256
FLOPS = 2 * D * Q * T * 3 + 2 * Q * E * I

F32 = mybir.dt.float32
BF16 = mybir.dt.bfloat16
I32 = mybir.dt.int32
U32 = mybir.dt.uint32
U16 = mybir.dt.uint16
U8 = mybir.dt.uint8
FP8X4 = mybir.dt.float8_e4m3fn_x4
FP4X4 = mybir.dt.float4_e2m1fn_x4
COPY = mybir.ActivationFunctionType.Copy
MULT = mybir.AluOpType.mult
ADD = mybir.AluOpType.add
MAX = mybir.AluOpType.max

P = 128
PACK = 4
BANK = 512
HALF = I // 2
LAST = PACK - 1


def tile_attend_twocourts_threeq_mixed_kernel(
    tc, query, query2, keys_words, keys_scales, notes_words, notes_scales, users_words, users_scales,
    lam, rowf, mix_words, mix_scales, offs, offs2, offs3, offs4, offs5, out,
):
    nc = tc.nc
    with ExitStack() as ctx:
        held = ctx.enter_context(tc.tile_pool(name="held", bufs=1))
        ring4 = ctx.enter_context(tc.tile_pool(name="ring4", bufs=4))
        psum = ctx.enter_context(tc.psum_pool(name="psum", bufs=1))
        turn_banks = [psum.tile([P, BANK], F32, name="turn%d" % k) for k in range(2)]
        last_banks = [psum.tile([P, BANK], F32, name="last%d" % k) for k in range(2)]

        def load_list(src, name):
            tile = held.tile([P, I // 16], U16, name=name)
            nc.sync.dma_start(tile[:], src)
            return tile

        def zeroed_scales(width, name, engine):
            tile = held.tile([P, width], U8, name=name, align_bytes=64)
            engine.memset(tile[:].bitcast(I32), 0)
            return tile

        def load_scales(tile, src):
            for quad in range(4):
                nc.sync.dma_start(
                    tile[32 * quad : 32 * quad + 4, :].bitcast(I32), src[0, 4 * quad : 4 * quad + 4, :].bitcast(I32)
                )

        def load_fp4_words(src, width, name):
            tile = held.tile([P, 2 * width], U8, name=name, align_bytes=64)
            nc.sync.dma_start(tile[:].bitcast(I32), src[0].bitcast(I32))
            return tile

        def load_query_half(src, half, name):
            tile = held.tile([P, PACK, Q // 2], F32, name=name, tag=name)
            nc.sync.dma_start(
                tile[:], src.rearrange("(p j) q -> p j q", j=PACK)[:, :, half * (Q // 2) : (half + 1) * (Q // 2)]
            )
            return tile

        notes_s = zeroed_scales(T, "notes_s", nc.gpsimd)
        keys_s = zeroed_scales(T, "keys_s", nc.vector)
        users_s = zeroed_scales(T, "users_s", nc.vector)
        mix_s = zeroed_scales(E, "mix_s", nc.vector)
        f1 = held.tile([P, T], F32, name="f1")
        f2 = [held.tile([P, T], F32, name="f2_first")]
        nc.vector.memset(f2[0][:], 0.0)
        nc.gpsimd.memset(f1[:], 0.0)

        q_raw = [load_query_half(query, half, "q_raw%d" % half) for half in range(2)]
        notes_w = load_fp4_words(notes_words, T, "notes_w")
        load_scales(notes_s, notes_scales)
        list3 = load_list(offs3, "list3")
        list4 = load_list(offs4, "list4")
        keys_w = held.tile([P, T], U32, name="keys_w", align_bytes=64)
        nc.sync.dma_start(keys_w[:].bitcast(I32), keys_words[0].rearrange("p n r -> p (n r)").bitcast(I32))
        load_scales(keys_s, keys_scales)
        list1 = load_list(offs, "list1")
        list2 = load_list(offs2, "list2")
        q2_raw = [load_query_half(query2, half, "q2_raw%d" % half) for half in range(2)]
        lam_sb = held.tile([P, PACK], F32, name="lam_sb")
        nc.sync.dma_start(lam_sb[:], lam.rearrange("(p t) o -> p (t o)", t=PACK))
        users_w = load_fp4_words(users_words, T, "users_w")
        load_scales(users_s, users_scales)
        list5 = load_list(offs5, "list5")
        rowf_sb = held.tile([P, PACK], F32, name="rowf_sb")
        nc.sync.dma_start(rowf_sb[:], rowf.rearrange("(p t) o -> p (t o)", t=PACK))
        mix_w = load_fp4_words(mix_words, E, "mix_w")
        load_scales(mix_s, mix_scales)

        q_first = held.tile([P, P, PACK], BF16, name="q_first", align_bytes=64)
        q_rest = held.tile([P, LAST, P, PACK], BF16, name="q_rest", align_bytes=64)
        r = held.tile([P, T], F32, name="r", align_bytes=64)
        q2_all = r[:].bitcast(BF16).rearrange("p (t m j) -> p t m j", t=PACK, j=PACK)
        for half in range(2):
            ms = slice(half * 64, (half + 1) * 64)
            dealt = q_raw[half][:].rearrange("p j (m t) -> p m t j", t=PACK)
            nc.vector.tensor_copy(q_first[:, ms, :], dealt[:, :, 0, :])
            nc.scalar.copy(q_rest[:, :, ms, :].rearrange("p t m j -> p m t j"), dealt[:, :, 1:PACK, :])
        first_c = held.tile([P, P], U32, name="first_c", align_bytes=64)
        first_s = held.tile([P, P], U8, name="first_s", align_bytes=64)
        rest_c = held.tile([P, LAST * P], U32, name="rest_c", align_bytes=64)
        rest_s = held.tile([P, LAST * P], U8, name="rest_s", align_bytes=64)
        nc.vector.quantize_mx(first_c[:].bitcast(FP8X4), first_s[:], q_first[:].rearrange("p m j -> p (m j)"))
        nc.vector.quantize_mx(rest_c[:].bitcast(FP8X4), rest_s[:], q_rest[:].rearrange("p t m j -> p (t m j)"))
        q_ops = [(first_c[:], first_s[:])] + [
            (rest_c[:, k * P : (k + 1) * P], rest_s[:, k * P : (k + 1) * P]) for k in range(LAST)
        ]
        q2_c = held.tile([P, Q], U32, name="q2_c", align_bytes=64)
        q2_s = held.tile([P, Q], U8, name="q2_s", align_bytes=64)

        def quantise_query2():
            for half in range(2):
                ms = slice(half * 64, (half + 1) * 64)
                nc.gpsimd.tensor_scalar(
                    q2_all[:, :, ms, :].rearrange("p t m j -> p m t j"),
                    q2_raw[half][:].rearrange("p j (m t) -> p m t j", t=PACK),
                    1.0, 0.0, MULT, ADD,
                )
            nc.vector.quantize_mx(q2_c[:].bitcast(FP8X4), q2_s[:], r[:].bitcast(BF16))
            f2.append(held.tile([P, T], F32, name="f2_second", tag="q2_raw1"))
            nc.gpsimd.memset(f2[1][:], 0.0)

        def scores(banks, rows, words, scales):
            for k in range(2):
                nc.tensor.matmul_mx(
                    banks[k][:], lhsT=rows[0].bitcast(FP8X4), lhsT_scale=rows[1],
                    rhs=words(k), rhs_scale=scales[:, k * BANK : (k + 1) * BANK], start=True, stop=True,
                )

        def notes_cols(k):
            return notes_w[:, 2 * k * BANK : 2 * (k + 1) * BANK].bitcast(FP4X4)

        def users_cols(k):
            return users_w[:, 2 * k * BANK : 2 * (k + 1) * BANK].bitcast(FP4X4)

        def keys_cols(k):
            return keys_w[:, k * BANK : (k + 1) * BANK].bitcast(FP8X4)

        a_sb = held.tile([P, T], F32, name="a_sb")
        b_sb = held.tile([P, T], F32, name="b_sb")
        c0 = [held.tile([P, T], F32, name="c0_%d" % k) for k in range(2)]
        cc_tiles = [held.tile([P, T], F32, name="cc%d" % k) for k in range(2)]
        slots = [held.tile([P, I], F32, name="slots%d" % k) for k in range(11)]
        b_picked = slots[0:4]
        a_picked = slots[4:8]
        g_tiles = [slots[8], slots[9], slots[10], slots[10]]

        def empty(banks, whole):
            for k in range(2):
                nc.scalar.copy(whole[:, k * BANK : (k + 1) * BANK], banks[k][:])

        def pick_notes(t):
            if t == 0:
                quarter = T // 4
                for k, bank in enumerate(turn_banks + last_banks):
                    cols = slice(k * quarter, (k + 1) * quarter)
                    nc.tensor.matmul_mx(
                        bank[:, :quarter], lhsT=q_ops[t][0].bitcast(FP8X4), lhsT_scale=q_ops[t][1],
                        rhs=notes_w[:, 2 * k * quarter : 2 * (k + 1) * quarter].bitcast(FP4X4),
                        rhs_scale=notes_s[:, cols], start=True, stop=True,
                    )
                    if k % 2 == 0:
                        nc.scalar.copy(b_sb[:, cols], bank[:, :quarter])
                    else:
                        nc.vector.tensor_copy(b_sb[:, cols], bank[:, :quarter])
                nc.scalar.activation(b_picked[t][:, :HALF], b_sb[:].indirect(list3[:, :16]), COPY)
                nc.vector.tensor_copy(b_picked[t][:, HALF:], b_sb[:].indirect(list3[:, 16:]))
            else:
                scores(turn_banks, q_ops[t], notes_cols, notes_s)
                empty(turn_banks, b_sb)
                nc.scalar.activation(b_picked[t][:], b_sb[:].indirect(list3[:]), COPY)

        def score_keys(t):
            scores(turn_banks, q_ops[t], keys_cols, keys_s)
            empty(turn_banks, a_sb)

        def pick_keys(t):
            nc.scalar.activation(a_picked[t][:], a_sb[:].indirect(list1[:]), COPY)

        def put(t):
            k = 1 if t == 2 else 0
            nc.vector.tensor_copy(f2[k][:].indirect(list4[:]), b_picked[t][:])
            nc.vector.tensor_copy(f1[:].indirect(list2[:]), a_picked[t][:])
            pieces = 2 if t == LAST else 1
            for piece in range(pieces):
                cols = slice(piece * T // pieces, (piece + 1) * T // pieces)
                nc.vector.scalar_tensor_tensor(
                    r[:, cols], f2[k][:, cols], lam_sb[:, t : t + 1], f1[:, cols], MULT, MAX
                )

        def score_users(t):
            rows = (q2_c[:, t * P : (t + 1) * P], q2_s[:, t * P : (t + 1) * P])
            scores(last_banks if t == LAST else turn_banks, rows, users_cols, users_s)
            if t < LAST:
                empty(turn_banks, c0[t % 2])

        def add_users(t):
            cc = cc_tiles[t // LAST]
            if t == LAST:
                for k in range(2):
                    cols = slice(k * BANK, (k + 1) * BANK)
                    nc.vector.tensor_tensor(cc[:, cols], r[:, cols], last_banks[k][:], ADD)
            else:
                nc.gpsimd.tensor_tensor(cc[:], r[:], c0[t % 2][:], ADD)

        gw = [held.tile([P, HALF, PACK], BF16, name="gw%d" % half, align_bytes=64) for half in range(2)]

        def weigh(t):
            factor = rowf_sb[:, t : t + 1]
            g = g_tiles[t]
            cc = cc_tiles[t // LAST]
            if t == LAST:
                nc.vector.tensor_copy(g[:, :HALF], cc[:].indirect(list5[:, :16]))
                nc.scalar.activation(g[:, HALF:], cc[:].indirect(list5[:, 16:]), COPY)
                nc.vector.tensor_scalar(gw[0][:, :, t], g[:, :HALF], factor, None, MULT)
                nc.scalar.activation(gw[1][:, :P, t], g[:, HALF : HALF + P], COPY, scale=factor)
                nc.vector.tensor_scalar(gw[1][:, P:, t], g[:, HALF + P :], factor, None, MULT)
            else:
                nc.scalar.activation(g[:], cc[:].indirect(list5[:]), COPY)

        def weigh_early(t):
            for half in range(2):
                nc.gpsimd.tensor_scalar(
                    gw[half][:, :, t], g_tiles[t][:, half * HALF : (half + 1) * HALF], rowf_sb[:, t : t + 1], 0.0, MULT, ADD
                )

        pick_notes(0)
        score_keys(0)
        pick_keys(0)
        quantise_query2()
        put(0)
        pick_notes(1)
        score_keys(1)
        pick_keys(1)
        score_users(0)
        for t in range(LAST):
            add_users(t)
            if t > 0:
                weigh_early(t - 1)
            put(t + 1)
            if t + 2 < PACK:
                pick_notes(t + 2)
                score_keys(t + 2)
                pick_keys(t + 2)
            score_users(t + 1)
            weigh(t)
        weigh_early(LAST - 1)
        add_users(LAST)
        weigh(LAST)

        for half in range(2):
            gw_c = held.tile([P, HALF], U32, name="gw_c%d" % half, align_bytes=64)
            gw_s = held.tile([P, HALF], U8, name="gw_s%d" % half, align_bytes=64)
            nc.vector.quantize_mx(gw_c[:].bitcast(FP8X4), gw_s[:], gw[half][:].rearrange("p i t -> p (i t)"))
            for c in range(E // P):
                bank = psum.tile([P, HALF], F32, name="y_bank%d%d" % (half, c))
                nc.tensor.matmul_mx(
                    bank[:], lhsT=mix_w[:, 2 * c * P : 2 * (c + 1) * P].bitcast(FP4X4),
                    lhsT_scale=mix_s[:, c * P : (c + 1) * P],
                    rhs=gw_c[:].bitcast(FP8X4), rhs_scale=gw_s[:], start=True, stop=True,
                )
                y = ring4.tile([P, HALF], F32, name="y")
                place = out[c * P : (c + 1) * P, half * HALF : (half + 1) * HALF]
                if c == half:
                    nc.scalar.copy(y[:], bank[:])
                    nc.scalar.dma_start(place, y[:])
                else:
                    nc.vector.tensor_copy(y[:], bank[:])
                    nc.sync.dma_start(place, y[:])
